import numpy as np
import ml_dtypes


def mxq(x, axis, fmt="e4m3"):
    dtype, down = {"e4m3": (ml_dtypes.float8_e4m3fn, 7), "e5m2": (ml_dtypes.float8_e5m2, 14)}[fmt]
    v = np.moveaxis(np.asarray(x, np.float32).astype(ml_dtypes.bfloat16).astype(np.float64), axis, -1)
    blocks = v.reshape(v.shape[:-1] + (-1, 32))
    amax = np.abs(blocks).max(-1, keepdims=True)
    byte = np.maximum(np.where(amax > 0, np.frexp(amax)[1] - 1 + 127, 0) - down, 1)
    scale = np.exp2(byte - 127.0)
    codes = (blocks / scale).astype(np.float32).astype(dtype).astype(np.float64)
    return np.moveaxis((codes * scale).reshape(v.shape), -1, axis)


WIDE = False


def mx_kscale(k):
    if not WIDE:
        return np.ones(k)
    levels = np.array([10, -10, 5, -5, 0])
    if k % 512:
        return np.exp2(np.random.permutation(np.resize(levels, k // 32))).repeat(32)
    a = np.empty((k // 512, 16))
    for p in range(k // 512):
        a[p, :8] = np.random.permutation(np.resize(levels, 8))
        for g in range(8):
            far = levels[np.abs(levels - a[p, g]) >= 10]
            a[p, g + 8] = far[np.random.randint(len(far))]
    return np.exp2(a.ravel()).repeat(32)


def f64(x):
    return np.asarray(x).astype(np.float64)


def striped(idx):
    return np.tile(idx.reshape(-1, 16).T, (8, 1)).astype(np.uint16)


def unstriped(offs):
    return offs[:16].T.reshape(-1).astype(np.int64)


def pack_weight(w):
    k, n = w.shape
    w = f64(np.asarray(w, np.float32).astype(ml_dtypes.bfloat16)).reshape(k // 32, 32, n)
    amax = np.abs(w).max(1)
    byte = np.clip(np.where(amax > 0, np.frexp(amax)[1] - 1 + 127 - 7, 1), 1, 254)
    scaled = (w * np.exp2(127.0 - byte)[:, None, :]).reshape(k, n).astype(np.float32)
    words = np.ascontiguousarray(scaled.reshape(k // 512, 128, 4, n).transpose(0, 1, 3, 2)).astype(ml_dtypes.float8_e4m3fn).view(np.uint8)
    return words, np.ascontiguousarray(byte.astype(np.uint8).reshape(k // 512, 16, n))


def unpack_weight(words, scales):
    g, p, n, _ = words.shape
    vals = np.ascontiguousarray(words).view(ml_dtypes.float8_e4m3fn).astype(np.float64) * np.repeat(np.exp2(scales.astype(np.float64) - 127.0), 8, axis=1)[..., None]
    return vals.transpose(0, 1, 3, 2).reshape(g * 512, n)


E2M1 = np.array([0.0, 0.5, 1.0, 1.5, 2.0, 3.0, 4.0, 6.0, -0.0, -0.5, -1.0, -1.5, -2.0, -3.0, -4.0, -6.0])


def pack_fp4(w):
    k, n = w.shape
    w = f64(np.asarray(w, np.float32).astype(ml_dtypes.bfloat16)).reshape(k // 32, 32, n)
    amax = np.abs(w).max(1)
    mant, ex = np.frexp(amax / 6.0)
    byte = np.clip(np.where(amax > 0, np.where(mant > 0.5, ex, ex - 1) + 127, 1), 1, 254)
    scaled = (w * np.exp2(127.0 - byte)[:, None, :]).reshape(k, n).astype(np.float32)
    c = np.ascontiguousarray(scaled.reshape(k // 512, 128, 4, n).transpose(0, 1, 3, 2)).astype(ml_dtypes.float4_e2m1fn).view(np.uint8) & 0xF
    words = (c[..., 0::2] | (c[..., 1::2] << 4)).reshape(k // 512, 128, 2 * n)
    return np.ascontiguousarray(words), np.ascontiguousarray(byte.astype(np.uint8).reshape(k // 512, 16, n))


def unpack_fp4(words, scales):
    g, _, n = scales.shape
    words = np.ascontiguousarray(words).reshape(g, 128, n, 2)
    nib = np.empty((g, 128, n, 4), np.uint8)
    nib[..., 0::2] = words & 0xF
    nib[..., 1::2] = words >> 4
    vals = E2M1[nib] * np.repeat(np.exp2(scales.astype(np.float64) - 127.0), 8, axis=1)[..., None]
    return vals.transpose(0, 1, 3, 2).reshape(g * 512, n)


def planes(y):
    n, m = y.shape
    v = y.astype(np.float32).astype(ml_dtypes.bfloat16).astype(np.float64).reshape(n // 32, 32, m)
    top = np.abs(v).max(1)
    byte = np.clip(np.where(top > 0, np.frexp(top)[1] - 1 + 127 - 7, 1), 1, 254)
    codes = (v * np.exp2(127.0 - byte)[:, None, :]).reshape(n, m).astype(np.float32).astype(ml_dtypes.float8_e4m3fn).view(np.uint8)
    words = codes.reshape(n // 512, 128, 4, m).transpose(0, 1, 3, 2)
    return np.ascontiguousarray(words), np.ascontiguousarray(byte.astype(np.uint8).reshape(n // 512, 16, m))


def silu(v):
    return v / (1.0 + np.exp(-np.maximum(v, -700.0)))


K, T, S, H, Z, W = 512, 2048, 512, 512, 512, 2048
P = 2 ** 7


def setup_inputs():
    n = np.random.standard_normal
    s = mx_kscale(K)[:, None]
    u = mx_kscale(H)
    packed_xT = pack_weight(n((K, T)) * s)
    packed_w1 = pack_fp4(n((K, H)) / np.sqrt(K) / s)
    packed_w2 = pack_fp4(n((K, H)) / np.sqrt(K) / s)
    packed_eT = pack_weight(n((K, W)) * s)
    packed_w3 = pack_fp4(n((K, H)) / np.sqrt(K) / s)
    return {
        "x_words": packed_xT[0],
        "x_scales": packed_xT[1],
        "w1_words": packed_w1[0],
        "w1_scales": packed_w1[1],
        "w2_words": packed_w2[0],
        "w2_scales": packed_w2[1],
        "e_words": packed_eT[0],
        "e_scales": packed_eT[1],
        "w3_words": packed_w3[0],
        "w3_scales": packed_w3[1],
        "unit": (np.random.uniform(0.6, 1.4, (H, 1)) * u[:, None]).astype(np.float32),
        "unit2": (np.random.uniform(0.6, 1.4, (H, 1)) / np.sqrt(H) / u[:, None]).astype(np.float32),
        "frq": (np.tile(np.random.uniform(-0.5, 0.5, W), (P, 1))).astype(np.float32),
        "offs": striped(np.random.permutation(T)[:S]),
        "obj": striped(np.random.permutation(W)[:Z]),
        "ctx1": striped(np.random.permutation(S)),
    }


def reference(x_words, x_scales, w1_words, w1_scales, w2_words, w2_scales, e_words, e_scales, w3_words, w3_scales, unit, unit2, frq, offs, obj, ctx1):
    xq = unpack_weight(x_words, x_scales)[:, unstriped(offs)]
    y = unpack_fp4(w1_words, w1_scales).T @ xq
    yr = unpack_fp4(w2_words, w2_scales).T @ xq
    rc = yr[:, unstriped(ctx1)]
    sub_ = y * (np.tanh(rc) + 1.0)
    hid = f64(unit) * sub_
    e_obj = unpack_weight(e_words, e_scales)[:, unstriped(obj)]
    ye = unpack_fp4(w3_words, w3_scales).T @ e_obj
    obj_ = silu(ye)
    hid2 = f64(unit2) * obj_
    sc = mxq(hid, 0, "e4m3").T @ mxq(hid2, 0, "e4m3")
    best4 = sc.reshape(len(sc), -1, 4).max(axis=2)
    dev = sc - np.repeat(best4, 4, axis=1)
    out_0 = (np.exp(1.5 * np.tanh(dev))) * (f64(frq)[:1][:, unstriped(obj)]) + 0.5 * sc
    return (out_0,) + planes(out_0)

@@ -1,0 +1,287 @@
+from contextlib import ExitStack
+
+import concourse.mybir as mybir
+from concourse.masks import make_identity
+
+F32 = mybir.dt.float32
+BF16 = mybir.dt.bfloat16
+I32 = mybir.dt.int32
+U32 = mybir.dt.uint32
+U16 = mybir.dt.uint16
+U8 = mybir.dt.uint8
+FP8X4 = mybir.dt.float8_e4m3fn_x4
+FP4X4 = mybir.dt.float4_e2m1fn_x4
+ACT = mybir.ActivationFunctionType
+ALU = mybir.AluOpType
+
+P = 128
+PACK = 4
+STORE = 2048
+PICKED = 512
+HIDDEN = 512
+CHUNK = 128
+CHUNKS = PICKED // CHUNK
+HALF = PICKED // 2
+GROUP = 4
+FOLD = STORE // P
+
+FLOPS = 4 * 2 * 512 * 512 * 512
+
+
+def load_scale_rows(queue, plane_words, scales):
+    rows = scales[0].bitcast(I32)
+    for q in range(4):
+        queue.dma_start(out=plane_words[32 * q : 32 * q + 4, :], in_=rows[4 * q : 4 * q + 4, :])
+
+
+def tile_picked_yscnrel_exp_po_kernel(
+    tc, x_words, x_scales, w1_words, w1_scales, w2_words, w2_scales, e_words, e_scales,
+    w3_words, w3_scales, unit, unit2, frq, offs, obj, ctx1, out_0, out_1, out_2,
+):
+    nc = tc.nc
+    with ExitStack() as ctx:
+        keep = ctx.enter_context(tc.tile_pool(name="keep", bufs=1))
+        work = ctx.enter_context(tc.tile_pool(name="work", bufs=CHUNKS))
+        psum = ctx.enter_context(tc.psum_pool(name="psum", bufs=1))
+
+        offs_list = keep.tile([P, PICKED // 16], U16)
+        obj_list = keep.tile([P, PICKED // 16], U16)
+        ctx_list = keep.tile([P, PICKED // 16], U16)
+        x_table = keep.tile([P, STORE], U32)
+        x_table_scales = keep.tile([P, STORE], U8)
+        e_table = keep.tile([P, STORE], U32)
+        e_table_scales = keep.tile([P, STORE], U8)
+        frq_table = keep.tile([P, STORE], F32)
+        w_raw = [keep.tile([P, HIDDEN // 2], I32, name=f"w_raw{w}") for w in range(3)]
+        w_raw_scales = [keep.tile([P, HIDDEN // 4], I32, name=f"w_raw_scales{w}") for w in range(3)]
+        unit_rows = keep.tile([P, P], F32)
+        frq_folded = keep.tile([P, FOLD], F32)
+        identity = keep.tile([P, P], F32)
+
+        nc.gpsimd.memset(x_table_scales[:].bitcast(I32), 0)
+        nc.vector.memset(w_raw_scales[1][:], 0)
+        nc.vector.memset(e_table_scales[:].bitcast(I32), 0)
+        nc.vector.memset(w_raw_scales[0][:], 0)
+        nc.vector.memset(w_raw_scales[2][:], 0)
+        make_identity(nc, identity[:])
+        nc.gpsimd.memset(unit_rows[:], 0.0)
+
+        def table_words(words):
+            return words[0].rearrange("p n t -> p (n t)").bitcast(I32)
+
+        for u, factors in enumerate((unit, unit2)):
+            nc.gpsimd.dma_start(
+                out=unit_rows[PACK * u : PACK * (u + 1), :].rearrange("t (g r) -> t g r", r=8),
+                in_=factors.rearrange("(g t r) o -> t g (r o)", t=PACK, r=8),
+            )
+        nc.sync.dma_start(out=frq_folded[:], in_=frq[0:1, :].rearrange("o (n m) -> (o n) m", m=FOLD))
+        nc.sync.dma_start(offs_list[:], offs)
+        load_scale_rows(nc.sync, x_table_scales[:].bitcast(I32), x_scales)
+        nc.sync.dma_start(obj_list[:], obj)
+        nc.sync.dma_start(out=x_table[:].bitcast(I32), in_=table_words(x_words))
+        nc.sync.dma_start(out=w_raw[1][:], in_=w2_words[0].bitcast(I32))
+        load_scale_rows(nc.sync, w_raw_scales[1][:], w2_scales)
+        nc.sync.dma_start(out=e_table[:].bitcast(I32), in_=table_words(e_words))
+        load_scale_rows(nc.sync, e_table_scales[:].bitcast(I32), e_scales)
+        nc.sync.dma_start(ctx_list[:], ctx1)
+        nc.sync.dma_start(out=w_raw[0][:], in_=w1_words[0].bitcast(I32))
+        load_scale_rows(nc.sync, w_raw_scales[0][:], w1_scales)
+        nc.sync.dma_start(out=w_raw[2][:], in_=w3_words[0].bitcast(I32))
+        load_scale_rows(nc.sync, w_raw_scales[2][:], w3_scales)
+
+        frq_lines = frq_table[:].rearrange("p (n b m) -> p b n m", b=FOLD // 4, m=4)
+        for b in range(FOLD // 4):
+            spread = psum.tile([P, 4, P], F32, name=f"spread{b}", tag=f"bank_a{b}")
+            for m in range(4):
+                column = frq_folded[:, 4 * b + m : 4 * b + m + 1]
+                nc.tensor.transpose(spread[:, m, :], column.to_broadcast([P, P]), identity[:])
+            nc.scalar.activation(frq_lines[:, b], spread[:].rearrange("p m n -> p n m"), ACT.Copy)
+        frq_picked = keep.tile([P, PICKED], F32)
+        nc.scalar.activation(frq_picked[:], frq_table[:].indirect(obj_list[:]), ACT.Copy)
+
+        unit_turned = psum.tile([P, P], F32, tag="bank_b3")
+        nc.tensor.transpose(unit_turned[:], unit_rows[:], identity[:])
+        units = keep.tile([P, 2 * PACK], F32)
+        nc.vector.tensor_copy(out=units[:], in_=unit_turned[:, 0 : 2 * PACK])
+
+        def deal_weight(w):
+            codes = keep.tile([P, 2 * HIDDEN], U8, name=f"w_codes{w}", align_bytes=64)
+            scales = keep.tile([P, HIDDEN], U8, name=f"w_scales{w}", align_bytes=64)
+            nc.gpsimd.tensor_copy(
+                out=codes[:].bitcast(I32).rearrange("p (t g r) -> p t g r", t=PACK, r=4),
+                in_=w_raw[w][:].rearrange("p (g t r) -> p t g r", t=PACK, r=4),
+            )
+            nc.gpsimd.tensor_copy(
+                out=scales[:].bitcast(I32).rearrange("p (t g r) -> p t g r", t=PACK, r=2),
+                in_=w_raw_scales[w][:].rearrange("p (g t r) -> p t g r", t=PACK, r=2),
+            )
+            return codes, scales
+
+        def weight_product(out, weight, t, picked, cols):
+            w_codes, w_scales = weight
+            codes, scales = picked
+            nc.tensor.matmul_mx(
+                out=out,
+                lhsT=w_codes[:, 2 * P * t : 2 * P * (t + 1)].bitcast(FP4X4),
+                lhsT_scale=w_scales[:, P * t : P * (t + 1)],
+                rhs=codes[:, cols].bitcast(FP8X4),
+                rhs_scale=scales[:, cols],
+                start=True,
+                stop=True,
+            )
+
+        def pick(name, table, table_scales, entries):
+            codes = keep.tile([P, PICKED], U32, name=f"{name}_codes", align_bytes=64)
+            scales = keep.tile([P, PICKED], U8, name=f"{name}_scales", align_bytes=64)
+            if name == "x":
+                nc.vector.tensor_copy(scales[:], table_scales[:].indirect(entries[:]))
+            nc.vector.tensor_copy(codes[:], table[:].indirect(entries[:]))
+            if name != "x":
+                nc.vector.tensor_copy(scales[:], table_scales[:].indirect(entries[:]))
+            return codes, scales
+
+        chunk_cols = [slice(CHUNK * c, CHUNK * (c + 1)) for c in range(CHUNKS)]
+
+        x_picked = pick("x", x_table, x_table_scales, offs_list)
+        w2 = deal_weight(1)
+        context_tanh = []
+        for t in range(PACK):
+            yr = psum.tile([P, PICKED], F32, name=f"yr{t}", tag=f"bank_a{t}")
+            weight_product(yr[:], w2, t, x_picked, slice(0, PICKED))
+            tanh_t = work.tile([P, PICKED], F32, name="tanh_t")
+            nc.scalar.activation(tanh_t[:], yr[:], ACT.Tanh)
+            context_tanh.append(tanh_t)
+
+        gates = []
+        for t in range(PACK):
+            gate = work.tile([P, PICKED], F32, name="gate")
+            nc.gpsimd.tensor_scalar(
+                gate[:], context_tanh[t][:], units[:, t : t + 1], units[:, t : t + 1], ALU.mult, ALU.add
+            )
+            gates.append(gate)
+
+        e_picked = pick("e", e_table, e_table_scales, obj_list)
+        w1 = deal_weight(0)
+        y_banks = []
+        for c in range(CHUNKS):
+            y = psum.tile([P, PACK, CHUNK], F32, name=f"y{c}", tag=f"bank_b{c}")
+            for t in range(PACK):
+                weight_product(y[:, t, :], w1, t, x_picked, chunk_cols[c])
+            y_banks.append(y)
+
+        w3 = deal_weight(2)
+        ye_banks = []
+        for c in range(CHUNKS):
+            ye = psum.tile([P, PACK, CHUNK], F32, name=f"ye{c}", tag=f"bank_a{c}")
+            for t in range(PACK):
+                weight_product(ye[:, t, :], w3, t, e_picked, chunk_cols[c])
+            ye_banks.append(ye)
+
+        hid = keep.tile([P, PACK, P, PACK], BF16, align_bytes=64)
+        for h in range(2):
+            fetched = keep.tile([P, PACK, HALF], F32, name=f"fetched{h}")
+            entries = ctx_list[:, HALF // 16 * h : HALF // 16 * (h + 1)]
+            for t in range(PACK):
+                if t <= h:
+                    nc.vector.tensor_copy(fetched[:, t, :], gates[t][:].indirect(entries))
+                else:
+                    nc.scalar.activation(fetched[:, t, :], gates[t][:].indirect(entries), ACT.Copy)
+            for c in (2 * h, 2 * h + 1):
+                within = slice(CHUNK * (c % 2), CHUNK * (c % 2 + 1))
+                nc.vector.tensor_tensor(
+                    hid[:, :, 32 * c : 32 * (c + 1), :].rearrange("p r m t -> p m r t"),
+                    y_banks[c][:].rearrange("p t (m r) -> p m r t", r=PACK),
+                    fetched[:, :, within].rearrange("p t (m r) -> p m r t", r=PACK),
+                    ALU.mult,
+                )
+        hid_codes = keep.tile([P, PICKED], U32, align_bytes=64)
+        hid_scales = keep.tile([P, PICKED], U8, align_bytes=64)
+        nc.vector.quantize_mx(
+            out=hid_codes[:].bitcast(FP8X4), scales=hid_scales[:], in_=hid[:].rearrange("p r m t -> p (r m t)")
+        )
+
+        silus = []
+        for c in range(CHUNKS):
+            silu = work.tile([P, CHUNK, PACK], F32, name="silu")
+            nc.scalar.activation(silu[:], ye_banks[c][:].rearrange("p t n -> p n t"), ACT.Silu)
+            silus.append(silu)
+
+        out_rows = out_0.rearrange("(p r) e -> p r e", r=PACK)
+        out_words = out_1[0].rearrange("p n t -> p (n t)").bitcast(I32)
+        out_scales = keep.tile([P, PICKED], U8, align_bytes=64)
+
+        def object_codes(c):
+            hid2 = work.tile([P, CHUNK, PACK], BF16, name="hid2", align_bytes=64)
+            nc.vector.tensor_tensor(
+                hid2[:],
+                silus[c][:],
+                units[:, PACK : 2 * PACK].unsqueeze(1).to_broadcast([P, CHUNK, PACK]),
+                ALU.mult,
+            )
+            hid2_codes = work.tile([P, CHUNK], U32, name="hid2_codes", align_bytes=64)
+            hid2_scales = work.tile([P, CHUNK], U8, name="hid2_scales", align_bytes=64)
+            nc.vector.quantize_mx(
+                out=hid2_codes[:].bitcast(FP8X4), scales=hid2_scales[:], in_=hid2[:].rearrange("p n t -> p (n t)")
+            )
+            return hid2_codes, hid2_scales
+
+        def score(c, hid2_codes, hid2_scales):
+            sc = psum.tile([P, PACK, CHUNK], F32, name=f"sc{c}", tag=f"bank_b{c}")
+            for r in range(PACK):
+                nc.tensor.matmul_mx(
+                    out=sc[:, r, :],
+                    lhsT=hid_codes[:, P * r : P * (r + 1)].bitcast(FP8X4),
+                    lhsT_scale=hid_scales[:, P * r : P * (r + 1)],
+                    rhs=hid2_codes[:].bitcast(FP8X4),
+                    rhs_scale=hid2_scales[:],
+                    start=True,
+                    stop=True,
+                )
+            return sc
+
+        def weigh(c, sc):
+            groups = sc[:].rearrange("p r (z d) -> p (r z) d", d=GROUP)
+            best = work.tile([P, P], F32, name="best")
+            nc.vector.tensor_reduce(best[:], groups, mybir.AxisListType.X, ALU.max)
+            dev = work.tile([P, P, GROUP], F32, name="dev")
+            nc.vector.tensor_tensor(dev[:], groups, best[:].unsqueeze(2).to_broadcast([P, P, GROUP]), ALU.subtract)
+            dev_tanh = work.tile([P, PACK * CHUNK], F32, name="dev_tanh")
+            nc.scalar.activation(dev_tanh[:], dev[:].rearrange("p g d -> p (g d)"), ACT.Tanh)
+            boost = work.tile([P, PACK, CHUNK], F32, name="boost")
+            nc.scalar.activation(boost[:].rearrange("p r n -> p (r n)"), dev_tanh[:], ACT.Exp, scale=1.5)
+            prior = work.tile([P, PACK, CHUNK], F32, name="prior")
+            nc.vector.tensor_tensor(
+                prior[:], boost[:], frq_picked[:, chunk_cols[c]].unsqueeze(1).to_broadcast([P, PACK, CHUNK]), ALU.mult
+            )
+            return prior
+
+        def hand_out(c, sc, prior):
+            result = work.tile([P, PACK, CHUNK], F32, name="result")
+            nc.vector.scalar_tensor_tensor(
+                result[:].rearrange("p r n -> p (r n)"),
+                sc[:].rearrange("p r n -> p (r n)"),
+                0.5,
+                prior[:].rearrange("p r n -> p (r n)"),
+                ALU.mult,
+                ALU.add,
+            )
+            nc.sync.dma_start(out=out_rows[:, :, chunk_cols[c]], in_=result[:])
+            rounded = work.tile([P, CHUNK, PACK], BF16, name="rounded", align_bytes=64)
+            nc.scalar.activation(rounded[:], result[:].rearrange("p r n -> p n r"), ACT.Copy)
+            out_codes = work.tile([P, CHUNK], U32, name="out_codes", align_bytes=64)
+            nc.vector.quantize_mx(
+                out=out_codes[:].bitcast(FP8X4),
+                scales=out_scales[:, chunk_cols[c]],
+                in_=rounded[:].rearrange("p n r -> p (n r)"),
+            )
+            nc.sync.dma_start(out=out_words[:, chunk_cols[c]], in_=out_codes[:].bitcast(I32))
+
+        scores = [score(c, *object_codes(c)) for c in range(CHUNKS)]
+        priors = [weigh(c, scores[c]) for c in range(CHUNKS)]
+        for c in range(CHUNKS):
+            hand_out(c, scores[c], priors[c])
+        scale_rows = out_2[0].bitcast(I32)
+        for q in range(4):
+            nc.sync.dma_start(
+                out=scale_rows[4 * q : 4 * q + 4, :], in_=out_scales[32 * q : 32 * q + 4, :].bitcast(I32)
+            )

@@ -23,15 +23,14 @@ CHUNK = 128
 CHUNKS = PICKED // CHUNK
 HALF = PICKED // 2
 GROUP = 4
-FOLD = STORE // P
 
 FLOPS = 4 * 2 * 512 * 512 * 512
 
 
-def load_scale_rows(queue, plane_words, scales):
+def load_scale_rows(nc, plane_words, scales):
     rows = scales[0].bitcast(I32)
     for q in range(4):
-        queue.dma_start(out=plane_words[32 * q : 32 * q + 4, :], in_=rows[4 * q : 4 * q + 4, :])
+        nc.sync.dma_start(out=plane_words[32 * q : 32 * q + 4, :], in_=rows[4 * q : 4 * q + 4, :])
 
 
 def tile_picked_yscnrel_exp_po_kernel(
@@ -49,69 +48,64 @@ def tile_picked_yscnrel_exp_po_kernel(
         ctx_list = keep.tile([P, PICKED // 16], U16)
         x_table = keep.tile([P, STORE], U32)
         x_table_scales = keep.tile([P, STORE], U8)
-        e_table = keep.tile([P, STORE], U32)
+        e_table = keep.tile([P, STORE], U32, tag="e_table")
         e_table_scales = keep.tile([P, STORE], U8)
         frq_table = keep.tile([P, STORE], F32)
         w_raw = [keep.tile([P, HIDDEN // 2], I32, name=f"w_raw{w}") for w in range(3)]
         w_raw_scales = [keep.tile([P, HIDDEN // 4], I32, name=f"w_raw_scales{w}") for w in range(3)]
         unit_rows = keep.tile([P, P], F32)
-        frq_folded = keep.tile([P, FOLD], F32)
         identity = keep.tile([P, P], F32)
 
         nc.gpsimd.memset(x_table_scales[:].bitcast(I32), 0)
+        nc.vector.memset(unit_rows[:], 0.0)
         nc.vector.memset(w_raw_scales[1][:], 0)
         nc.vector.memset(e_table_scales[:].bitcast(I32), 0)
         nc.vector.memset(w_raw_scales[0][:], 0)
         nc.vector.memset(w_raw_scales[2][:], 0)
         make_identity(nc, identity[:])
-        nc.gpsimd.memset(unit_rows[:], 0.0)
 
         def table_words(words):
             return words[0].rearrange("p n t -> p (n t)").bitcast(I32)
 
-        for u, factors in enumerate((unit, unit2)):
-            nc.gpsimd.dma_start(
+        def load_unit(queue, u, factors):
+            queue.dma_start(
                 out=unit_rows[PACK * u : PACK * (u + 1), :].rearrange("t (g r) -> t g r", r=8),
                 in_=factors.rearrange("(g t r) o -> t g (r o)", t=PACK, r=8),
             )
-        nc.sync.dma_start(out=frq_folded[:], in_=frq[0:1, :].rearrange("o (n m) -> (o n) m", m=FOLD))
+
         nc.sync.dma_start(offs_list[:], offs)
-        load_scale_rows(nc.sync, x_table_scales[:].bitcast(I32), x_scales)
         nc.sync.dma_start(obj_list[:], obj)
+        load_unit(nc.scalar, 0, unit)
+        load_scale_rows(nc, x_table_scales[:].bitcast(I32), x_scales)
         nc.sync.dma_start(out=x_table[:].bitcast(I32), in_=table_words(x_words))
         nc.sync.dma_start(out=w_raw[1][:], in_=w2_words[0].bitcast(I32))
-        load_scale_rows(nc.sync, w_raw_scales[1][:], w2_scales)
+        load_scale_rows(nc, w_raw_scales[1][:], w2_scales)
+        load_unit(nc.sync, 1, unit2)
         nc.sync.dma_start(out=e_table[:].bitcast(I32), in_=table_words(e_words))
-        load_scale_rows(nc.sync, e_table_scales[:].bitcast(I32), e_scales)
-        nc.sync.dma_start(ctx_list[:], ctx1)
         nc.sync.dma_start(out=w_raw[0][:], in_=w1_words[0].bitcast(I32))
-        load_scale_rows(nc.sync, w_raw_scales[0][:], w1_scales)
+        load_scale_rows(nc, w_raw_scales[0][:], w1_scales)
+        load_scale_rows(nc, e_table_scales[:].bitcast(I32), e_scales)
         nc.sync.dma_start(out=w_raw[2][:], in_=w3_words[0].bitcast(I32))
-        load_scale_rows(nc.sync, w_raw_scales[2][:], w3_scales)
+        load_scale_rows(nc, w_raw_scales[2][:], w3_scales)
+        nc.sync.dma_start(ctx_list[:], ctx1)
+        nc.sync.dma_start(out=frq_table[:], in_=frq)
 
-        frq_lines = frq_table[:].rearrange("p (n b m) -> p b n m", b=FOLD // 4, m=4)
-        for b in range(FOLD // 4):
-            spread = psum.tile([P, 4, P], F32, name=f"spread{b}", tag=f"bank_a{b}")
-            for m in range(4):
-                column = frq_folded[:, 4 * b + m : 4 * b + m + 1]
-                nc.tensor.transpose(spread[:, m, :], column.to_broadcast([P, P]), identity[:])
-            nc.scalar.activation(frq_lines[:, b], spread[:].rearrange("p m n -> p n m"), ACT.Copy)
-        frq_picked = keep.tile([P, PICKED], F32)
-        nc.scalar.activation(frq_picked[:], frq_table[:].indirect(obj_list[:]), ACT.Copy)
 
         unit_turned = psum.tile([P, P], F32, tag="bank_b3")
         nc.tensor.transpose(unit_turned[:], unit_rows[:], identity[:])
         units = keep.tile([P, 2 * PACK], F32)
         nc.vector.tensor_copy(out=units[:], in_=unit_turned[:, 0 : 2 * PACK])
+        table_warmup = keep.tile([P, 1], F32)
+        nc.scalar.activation(table_warmup[:], identity[:, 0:1], ACT.Silu)
 
         def deal_weight(w):
             codes = keep.tile([P, 2 * HIDDEN], U8, name=f"w_codes{w}", align_bytes=64)
             scales = keep.tile([P, HIDDEN], U8, name=f"w_scales{w}", align_bytes=64)
-            nc.gpsimd.tensor_copy(
+            nc.vector.tensor_copy(
                 out=codes[:].bitcast(I32).rearrange("p (t g r) -> p t g r", t=PACK, r=4),
                 in_=w_raw[w][:].rearrange("p (g t r) -> p t g r", t=PACK, r=4),
             )
-            nc.gpsimd.tensor_copy(
+            nc.vector.tensor_copy(
                 out=scales[:].bitcast(I32).rearrange("p (t g r) -> p t g r", t=PACK, r=2),
                 in_=w_raw_scales[w][:].rearrange("p (g t r) -> p t g r", t=PACK, r=2),
             )
@@ -152,78 +146,71 @@ def tile_picked_yscnrel_exp_po_kernel(
             nc.scalar.activation(tanh_t[:], yr[:], ACT.Tanh)
             context_tanh.append(tanh_t)
 
-        gates = []
-        for t in range(PACK):
-            gate = work.tile([P, PICKED], F32, name="gate")
-            nc.gpsimd.tensor_scalar(
-                gate[:], context_tanh[t][:], units[:, t : t + 1], units[:, t : t + 1], ALU.mult, ALU.add
-            )
-            gates.append(gate)
-
         e_picked = pick("e", e_table, e_table_scales, obj_list)
-        w1 = deal_weight(0)
-        y_banks = []
-        for c in range(CHUNKS):
-            y = psum.tile([P, PACK, CHUNK], F32, name=f"y{c}", tag=f"bank_b{c}")
-            for t in range(PACK):
-                weight_product(y[:, t, :], w1, t, x_picked, chunk_cols[c])
-            y_banks.append(y)
+        gates = keep.tile([P, PACK, PICKED], F32, tag="e_table")
+        for t in range(PACK):
+            nc.vector.tensor_scalar(
+                gates[:, t, :], context_tanh[t][:], units[:, t : t + 1], units[:, t : t + 1], ALU.mult, ALU.add
+            )
 
-        w3 = deal_weight(2)
-        ye_banks = []
-        for c in range(CHUNKS):
-            ye = psum.tile([P, PACK, CHUNK], F32, name=f"ye{c}", tag=f"bank_a{c}")
+        def chunk_product(name, weight, picked, c, bank):
+            product = psum.tile([P, PACK, CHUNK], F32, name=f"{name}{c}", tag=bank)
             for t in range(PACK):
-                weight_product(ye[:, t, :], w3, t, e_picked, chunk_cols[c])
-            ye_banks.append(ye)
+                weight_product(product[:, t, :], weight, t, picked, chunk_cols[c])
+            return product
 
         hid = keep.tile([P, PACK, P, PACK], BF16, align_bytes=64)
-        for h in range(2):
+
+        def subject_half(h, y_banks, vector_planes):
             fetched = keep.tile([P, PACK, HALF], F32, name=f"fetched{h}")
             entries = ctx_list[:, HALF // 16 * h : HALF // 16 * (h + 1)]
             for t in range(PACK):
-                if t <= h:
-                    nc.vector.tensor_copy(fetched[:, t, :], gates[t][:].indirect(entries))
+                if t < vector_planes:
+                    nc.vector.tensor_copy(fetched[:, t, :], gates[:, t, :].indirect(entries))
                 else:
-                    nc.scalar.activation(fetched[:, t, :], gates[t][:].indirect(entries), ACT.Copy)
-            for c in (2 * h, 2 * h + 1):
-                within = slice(CHUNK * (c % 2), CHUNK * (c % 2 + 1))
+                    nc.scalar.activation(fetched[:, t, :], gates[:, t, :].indirect(entries), ACT.Copy)
+            for i, y in enumerate(y_banks):
+                c = 2 * h + i
                 nc.vector.tensor_tensor(
                     hid[:, :, 32 * c : 32 * (c + 1), :].rearrange("p r m t -> p m r t"),
-                    y_banks[c][:].rearrange("p t (m r) -> p m r t", r=PACK),
-                    fetched[:, :, within].rearrange("p t (m r) -> p m r t", r=PACK),
+                    y[:].rearrange("p t (m r) -> p m r t", r=PACK),
+                    fetched[:, :, chunk_cols[i]].rearrange("p t (m r) -> p m r t", r=PACK),
                     ALU.mult,
                 )
-        hid_codes = keep.tile([P, PICKED], U32, align_bytes=64)
-        hid_scales = keep.tile([P, PICKED], U8, align_bytes=64)
-        nc.vector.quantize_mx(
-            out=hid_codes[:].bitcast(FP8X4), scales=hid_scales[:], in_=hid[:].rearrange("p r m t -> p (r m t)")
-        )
 
-        silus = []
-        for c in range(CHUNKS):
+        def object_codes(c, ye):
             silu = work.tile([P, CHUNK, PACK], F32, name="silu")
-            nc.scalar.activation(silu[:], ye_banks[c][:].rearrange("p t n -> p n t"), ACT.Silu)
-            silus.append(silu)
-
-        out_rows = out_0.rearrange("(p r) e -> p r e", r=PACK)
-        out_words = out_1[0].rearrange("p n t -> p (n t)").bitcast(I32)
-        out_scales = keep.tile([P, PICKED], U8, align_bytes=64)
-
-        def object_codes(c):
+            nc.scalar.activation(silu[:], ye[:].rearrange("p t n -> p n t"), ACT.Silu)
             hid2 = work.tile([P, CHUNK, PACK], BF16, name="hid2", align_bytes=64)
             nc.vector.tensor_tensor(
-                hid2[:],
-                silus[c][:],
-                units[:, PACK : 2 * PACK].unsqueeze(1).to_broadcast([P, CHUNK, PACK]),
-                ALU.mult,
+                hid2[:], silu[:], units[:, PACK : 2 * PACK].unsqueeze(1).to_broadcast([P, CHUNK, PACK]), ALU.mult
             )
             hid2_codes = work.tile([P, CHUNK], U32, name="hid2_codes", align_bytes=64)
             hid2_scales = work.tile([P, CHUNK], U8, name="hid2_scales", align_bytes=64)
             nc.vector.quantize_mx(
                 out=hid2_codes[:].bitcast(FP8X4), scales=hid2_scales[:], in_=hid2[:].rearrange("p n t -> p (n t)")
             )
-            return hid2_codes, hid2_scales
+            return hid2_codes, hid2_scales, silu
+
+        w1 = deal_weight(0)
+        w3 = deal_weight(2)
+        for h in range(2):
+            subject_half(h, [chunk_product("y", w1, x_picked, c, f"bank_b{c}") for c in (2 * h, 2 * h + 1)], h)
+        hid_codes = keep.tile([P, PICKED], U32, align_bytes=64)
+        hid_scales = keep.tile([P, PICKED], U8, align_bytes=64)
+        nc.vector.quantize_mx(
+            out=hid_codes[:].bitcast(FP8X4), scales=hid_scales[:], in_=hid[:].rearrange("p r m t -> p (r m t)")
+        )
+        objects = [object_codes(c, chunk_product("ye", w3, e_picked, c, f"bank_a{c}")) for c in range(CHUNKS)]
+
+        exp_warmup = keep.tile([P, 1], F32)
+        nc.scalar.activation(exp_warmup[:], objects[-1][2][:, 0, 0:1], ACT.Exp, scale=0.0)
+        frq_picked = keep.tile([P, PICKED], F32)
+        nc.scalar.activation(frq_picked[:], frq_table[:].indirect(obj_list[:]), ACT.Copy)
+
+        out_rows = out_0.rearrange("(p r) e -> p r e", r=PACK)
+        out_words = out_1[0].rearrange("p n t -> p (n t)").bitcast(I32)
+        out_scales = keep.tile([P, PICKED], U8, align_bytes=64)
 
         def score(c, hid2_codes, hid2_scales):
             sc = psum.tile([P, PACK, CHUNK], F32, name=f"sc{c}", tag=f"bank_b{c}")
@@ -276,7 +263,7 @@ def tile_picked_yscnrel_exp_po_kernel(
             )
             nc.sync.dma_start(out=out_words[:, chunk_cols[c]], in_=out_codes[:].bitcast(I32))
 
-        scores = [score(c, *object_codes(c)) for c in range(CHUNKS)]
+        scores = [score(c, *objects[c][:2]) for c in range(CHUNKS)]
         priors = [weigh(c, scores[c]) for c in range(CHUNKS)]
         for c in range(CHUNKS):
             hand_out(c, scores[c], priors[c])

@@ -67,20 +67,20 @@ def tile_picked_yscnrel_exp_po_kernel(
         def table_words(words):
             return words[0].rearrange("p n t -> p (n t)").bitcast(I32)
 
-        def load_unit(queue, u, factors):
-            queue.dma_start(
+        def load_unit(u, factors):
+            nc.sync.dma_start(
                 out=unit_rows[PACK * u : PACK * (u + 1), :].rearrange("t (g r) -> t g r", r=8),
                 in_=factors.rearrange("(g t r) o -> t g (r o)", t=PACK, r=8),
             )
 
         nc.sync.dma_start(offs_list[:], offs)
         nc.sync.dma_start(obj_list[:], obj)
-        load_unit(nc.scalar, 0, unit)
         load_scale_rows(nc, x_table_scales[:].bitcast(I32), x_scales)
+        load_unit(0, unit)
         nc.sync.dma_start(out=x_table[:].bitcast(I32), in_=table_words(x_words))
         nc.sync.dma_start(out=w_raw[1][:], in_=w2_words[0].bitcast(I32))
         load_scale_rows(nc, w_raw_scales[1][:], w2_scales)
-        load_unit(nc.sync, 1, unit2)
+        load_unit(1, unit2)
         nc.sync.dma_start(out=e_table[:].bitcast(I32), in_=table_words(e_words))
         nc.sync.dma_start(out=w_raw[0][:], in_=w1_words[0].bitcast(I32))
         load_scale_rows(nc, w_raw_scales[0][:], w1_scales)
@@ -178,33 +178,35 @@ def tile_picked_yscnrel_exp_po_kernel(
                     ALU.mult,
                 )
 
-        def object_codes(c, ye):
-            silu = work.tile([P, CHUNK, PACK], F32, name="silu")
-            nc.scalar.activation(silu[:], ye[:].rearrange("p t n -> p n t"), ACT.Silu)
-            hid2 = work.tile([P, CHUNK, PACK], BF16, name="hid2", align_bytes=64)
+        def object_half(h):
+            silu = keep.tile([P, HALF, PACK], F32, name=f"silu{h}")
+            for i in range(2):
+                ye = chunk_product("ye", w3, e_picked, 2 * h + i, f"bank_a{2 * h + i}")
+                nc.scalar.activation(silu[:, chunk_cols[i], :], ye[:].rearrange("p t n -> p n t"), ACT.Silu)
+            hid2 = keep.tile([P, HALF, PACK], BF16, name=f"hid2_{h}", align_bytes=64)
             nc.vector.tensor_tensor(
-                hid2[:], silu[:], units[:, PACK : 2 * PACK].unsqueeze(1).to_broadcast([P, CHUNK, PACK]), ALU.mult
+                hid2[:], silu[:], units[:, PACK : 2 * PACK].unsqueeze(1).to_broadcast([P, HALF, PACK]), ALU.mult
             )
-            hid2_codes = work.tile([P, CHUNK], U32, name="hid2_codes", align_bytes=64)
-            hid2_scales = work.tile([P, CHUNK], U8, name="hid2_scales", align_bytes=64)
+            codes = keep.tile([P, HALF], U32, name=f"hid2_codes{h}", align_bytes=64)
+            scales = keep.tile([P, HALF], U8, name=f"hid2_scales{h}", align_bytes=64)
             nc.vector.quantize_mx(
-                out=hid2_codes[:].bitcast(FP8X4), scales=hid2_scales[:], in_=hid2[:].rearrange("p n t -> p (n t)")
+                out=codes[:].bitcast(FP8X4), scales=scales[:], in_=hid2[:].rearrange("p n t -> p (n t)")
             )
-            return hid2_codes, hid2_scales, silu
+            return codes, scales, silu
 
         w1 = deal_weight(0)
         w3 = deal_weight(2)
         for h in range(2):
-            subject_half(h, [chunk_product("y", w1, x_picked, c, f"bank_b{c}") for c in (2 * h, 2 * h + 1)], h)
+            subject_half(h, [chunk_product("y", w1, x_picked, c, f"bank_b{c}") for c in (2 * h, 2 * h + 1)], 2 * h)
         hid_codes = keep.tile([P, PICKED], U32, align_bytes=64)
         hid_scales = keep.tile([P, PICKED], U8, align_bytes=64)
         nc.vector.quantize_mx(
             out=hid_codes[:].bitcast(FP8X4), scales=hid_scales[:], in_=hid[:].rearrange("p r m t -> p (r m t)")
         )
-        objects = [object_codes(c, chunk_product("ye", w3, e_picked, c, f"bank_a{c}")) for c in range(CHUNKS)]
+        objects = [object_half(h) for h in range(2)]
 
         exp_warmup = keep.tile([P, 1], F32)
-        nc.scalar.activation(exp_warmup[:], objects[-1][2][:, 0, 0:1], ACT.Exp, scale=0.0)
+        nc.scalar.activation(exp_warmup[:], objects[-1][2][:, HALF - 1, 0:1], ACT.Exp, scale=0.0)
         frq_picked = keep.tile([P, PICKED], F32)
         nc.scalar.activation(frq_picked[:], frq_table[:].indirect(obj_list[:]), ACT.Copy)
 
@@ -212,15 +214,16 @@ def tile_picked_yscnrel_exp_po_kernel(
         out_words = out_1[0].rearrange("p n t -> p (n t)").bitcast(I32)
         out_scales = keep.tile([P, PICKED], U8, align_bytes=64)
 
-        def score(c, hid2_codes, hid2_scales):
+        def score(c):
+            hid2_codes, hid2_scales = objects[c // 2][:2]
             sc = psum.tile([P, PACK, CHUNK], F32, name=f"sc{c}", tag=f"bank_b{c}")
             for r in range(PACK):
                 nc.tensor.matmul_mx(
                     out=sc[:, r, :],
                     lhsT=hid_codes[:, P * r : P * (r + 1)].bitcast(FP8X4),
                     lhsT_scale=hid_scales[:, P * r : P * (r + 1)],
-                    rhs=hid2_codes[:].bitcast(FP8X4),
-                    rhs_scale=hid2_scales[:],
+                    rhs=hid2_codes[:, chunk_cols[c % 2]].bitcast(FP8X4),
+                    rhs_scale=hid2_scales[:, chunk_cols[c % 2]],
                     start=True,
                     stop=True,
                 )
@@ -237,7 +240,8 @@ def tile_picked_yscnrel_exp_po_kernel(
             boost = work.tile([P, PACK, CHUNK], F32, name="boost")
             nc.scalar.activation(boost[:].rearrange("p r n -> p (r n)"), dev_tanh[:], ACT.Exp, scale=1.5)
             prior = work.tile([P, PACK, CHUNK], F32, name="prior")
-            nc.vector.tensor_tensor(
+            engine = nc.gpsimd if c < 2 else nc.vector
+            engine.tensor_tensor(
                 prior[:], boost[:], frq_picked[:, chunk_cols[c]].unsqueeze(1).to_broadcast([P, PACK, CHUNK]), ALU.mult
             )
             return prior
@@ -254,7 +258,10 @@ def tile_picked_yscnrel_exp_po_kernel(
             )
             nc.sync.dma_start(out=out_rows[:, :, chunk_cols[c]], in_=result[:])
             rounded = work.tile([P, CHUNK, PACK], BF16, name="rounded", align_bytes=64)
-            nc.scalar.activation(rounded[:], result[:].rearrange("p r n -> p n r"), ACT.Copy)
+            if c < CHUNKS - 1:
+                nc.scalar.activation(rounded[:], result[:].rearrange("p r n -> p n r"), ACT.Copy)
+            else:
+                nc.vector.tensor_copy(out=rounded[:], in_=result[:].rearrange("p r n -> p n r"))
             out_codes = work.tile([P, CHUNK], U32, name="out_codes", align_bytes=64)
             nc.vector.quantize_mx(
                 out=out_codes[:].bitcast(FP8X4),
@@ -263,12 +270,12 @@ def tile_picked_yscnrel_exp_po_kernel(
             )
             nc.sync.dma_start(out=out_words[:, chunk_cols[c]], in_=out_codes[:].bitcast(I32))
 
-        scores = [score(c, *objects[c][:2]) for c in range(CHUNKS)]
+        scores = [score(c) for c in range(CHUNKS)]
         priors = [weigh(c, scores[c]) for c in range(CHUNKS)]
         for c in range(CHUNKS):
             hand_out(c, scores[c], priors[c])
         scale_rows = out_2[0].bitcast(I32)
         for q in range(4):
-            nc.sync.dma_start(
+            (nc.scalar, nc.sync)[q % 2].dma_start(
                 out=scale_rows[4 * q : 4 * q + 4, :], in_=out_scales[32 * q : 32 * q + 4, :].bitcast(I32)
             )

@@ -29,8 +29,8 @@ FLOPS = 4 * 2 * 512 * 512 * 512
 
 def load_scale_rows(nc, plane_words, scales):
     rows = scales[0].bitcast(I32)
-    for q in range(4):
-        nc.sync.dma_start(out=plane_words[32 * q : 32 * q + 4, :], in_=rows[4 * q : 4 * q + 4, :])
+    for r in range(4):
+        nc.sync.dma_start(out=plane_words[r:P:32, :], in_=rows[r:16:4, :])
 
 
 def tile_picked_yscnrel_exp_po_kernel(
@@ -172,9 +172,9 @@ def tile_picked_yscnrel_exp_po_kernel(
             for i, y in enumerate(y_banks):
                 c = 2 * h + i
                 nc.vector.tensor_tensor(
-                    hid[:, :, 32 * c : 32 * (c + 1), :].rearrange("p r m t -> p m r t"),
-                    y[:].rearrange("p t (m r) -> p m r t", r=PACK),
-                    fetched[:, :, chunk_cols[i]].rearrange("p t (m r) -> p m r t", r=PACK),
+                    hid[:, :, 32 * c : 32 * (c + 1), :].rearrange("p r m t -> p m t r"),
+                    y[:].rearrange("p t (m r) -> p m t r", r=PACK),
+                    fetched[:, :, chunk_cols[i]].rearrange("p t (m r) -> p m t r", r=PACK),
                     ALU.mult,
                 )
 
@@ -258,10 +258,12 @@ def tile_picked_yscnrel_exp_po_kernel(
             )
             nc.sync.dma_start(out=out_rows[:, :, chunk_cols[c]], in_=result[:])
             rounded = work.tile([P, CHUNK, PACK], BF16, name="rounded", align_bytes=64)
+            woven = rounded[:].rearrange("p (n i) r -> p n r i", i=4)
+            by_rows = result[:].rearrange("p r (n i) -> p n r i", i=4)
             if c < CHUNKS - 1:
-                nc.scalar.activation(rounded[:], result[:].rearrange("p r n -> p n r"), ACT.Copy)
+                nc.scalar.activation(woven, by_rows, ACT.Copy)
             else:
-                nc.vector.tensor_copy(out=rounded[:], in_=result[:].rearrange("p r n -> p n r"))
+                nc.vector.tensor_copy(out=woven, in_=by_rows)
             out_codes = work.tile([P, CHUNK], U32, name="out_codes", align_bytes=64)
             nc.vector.quantize_mx(
                 out=out_codes[:].bitcast(FP8X4),

@@ -15,7 +15,7 @@ ACT = mybir.ActivationFunctionType
 ALU = mybir.AluOpType
 
 P = 128
-PACK = 4
+SLOTS = 4
 STORE = 2048
 PICKED = 512
 HIDDEN = 512
@@ -23,14 +23,21 @@ CHUNK = 128
 CHUNKS = PICKED // CHUNK
 HALF = PICKED // 2
 GROUP = 4
+LINE = 4
+W1 = 0
+W2 = 1
+W3 = 2
+
+VECTOR_FETCHES = (0, 1)
+GPSIMD_CHUNKS = 2
 
 FLOPS = 4 * 2 * 512 * 512 * 512
 
 
-def load_scale_rows(nc, plane_words, scales):
+def load_scale_rows(nc, scale_tile, scales):
     rows = scales[0].bitcast(I32)
-    for r in range(4):
-        nc.sync.dma_start(out=plane_words[r:P:32, :], in_=rows[r:16:4, :])
+    for a in range(4):
+        nc.sync.dma_start(out=scale_tile[a:P:32, :], in_=rows[a:16:4, :])
 
 
 def tile_picked_yscnrel_exp_po_kernel(
@@ -38,10 +45,10 @@ def tile_picked_yscnrel_exp_po_kernel(
     w3_words, w3_scales, unit, unit2, frq, offs, obj, ctx1, out_0, out_1, out_2,
 ):
     nc = tc.nc
-    with ExitStack() as ctx:
-        keep = ctx.enter_context(tc.tile_pool(name="keep", bufs=1))
-        work = ctx.enter_context(tc.tile_pool(name="work", bufs=CHUNKS))
-        psum = ctx.enter_context(tc.psum_pool(name="psum", bufs=1))
+    with ExitStack() as stack:
+        keep = stack.enter_context(tc.tile_pool(name="keep", bufs=1))
+        work = stack.enter_context(tc.tile_pool(name="work", bufs=CHUNKS))
+        psum = stack.enter_context(tc.psum_pool(name="psum", bufs=1))
 
         offs_list = keep.tile([P, PICKED // 16], U16)
         obj_list = keep.tile([P, PICKED // 16], U16)
@@ -51,17 +58,20 @@ def tile_picked_yscnrel_exp_po_kernel(
         e_table = keep.tile([P, STORE], U32, tag="e_table")
         e_table_scales = keep.tile([P, STORE], U8)
         frq_table = keep.tile([P, STORE], F32)
-        w_raw = [keep.tile([P, HIDDEN // 2], I32, name=f"w_raw{w}") for w in range(3)]
-        w_raw_scales = [keep.tile([P, HIDDEN // 4], I32, name=f"w_raw_scales{w}") for w in range(3)]
+        w_raw = [keep.tile([P, HIDDEN // 2], I32, name=f"w_raw{w}", tag=f"w_raw{w}") for w in range(3)]
+        w_raw_scales = [
+            keep.tile([P, HIDDEN // 4], I32, name=f"w_raw_scales{w}", tag=f"w_raw_scales{w}", align_bytes=64)
+            for w in range(3)
+        ]
         unit_rows = keep.tile([P, P], F32)
         identity = keep.tile([P, P], F32)
 
         nc.gpsimd.memset(x_table_scales[:].bitcast(I32), 0)
         nc.vector.memset(unit_rows[:], 0.0)
-        nc.vector.memset(w_raw_scales[1][:], 0)
+        nc.vector.memset(w_raw_scales[W2][:], 0)
         nc.vector.memset(e_table_scales[:].bitcast(I32), 0)
-        nc.vector.memset(w_raw_scales[0][:], 0)
-        nc.vector.memset(w_raw_scales[2][:], 0)
+        nc.vector.memset(w_raw_scales[W1][:], 0)
+        nc.vector.memset(w_raw_scales[W3][:], 0)
         make_identity(nc, identity[:])
 
         def table_words(words):
@@ -69,8 +79,8 @@ def tile_picked_yscnrel_exp_po_kernel(
 
         def load_unit(u, factors):
             nc.sync.dma_start(
-                out=unit_rows[PACK * u : PACK * (u + 1), :].rearrange("t (g r) -> t g r", r=8),
-                in_=factors.rearrange("(g t r) o -> t g (r o)", t=PACK, r=8),
+                out=unit_rows[SLOTS * u : SLOTS * (u + 1), :].rearrange("t (g r) -> t g r", r=8),
+                in_=factors.rearrange("(g t r) o -> t g (r o)", t=SLOTS, r=8),
             )
 
         nc.sync.dma_start(offs_list[:], offs)
@@ -78,114 +88,120 @@ def tile_picked_yscnrel_exp_po_kernel(
         load_scale_rows(nc, x_table_scales[:].bitcast(I32), x_scales)
         load_unit(0, unit)
         nc.sync.dma_start(out=x_table[:].bitcast(I32), in_=table_words(x_words))
-        nc.sync.dma_start(out=w_raw[1][:], in_=w2_words[0].bitcast(I32))
-        load_scale_rows(nc, w_raw_scales[1][:], w2_scales)
+        nc.sync.dma_start(out=w_raw[W2][:], in_=w2_words[0].bitcast(I32))
+        load_scale_rows(nc, w_raw_scales[W2][:], w2_scales)
         load_unit(1, unit2)
         nc.sync.dma_start(out=e_table[:].bitcast(I32), in_=table_words(e_words))
-        nc.sync.dma_start(out=w_raw[0][:], in_=w1_words[0].bitcast(I32))
-        load_scale_rows(nc, w_raw_scales[0][:], w1_scales)
-        load_scale_rows(nc, e_table_scales[:].bitcast(I32), e_scales)
-        nc.sync.dma_start(out=w_raw[2][:], in_=w3_words[0].bitcast(I32))
-        load_scale_rows(nc, w_raw_scales[2][:], w3_scales)
         nc.sync.dma_start(ctx_list[:], ctx1)
+        nc.sync.dma_start(out=w_raw[W1][:], in_=w1_words[0].bitcast(I32))
+        load_scale_rows(nc, w_raw_scales[W1][:], w1_scales)
+        load_scale_rows(nc, e_table_scales[:].bitcast(I32), e_scales)
+        nc.sync.dma_start(out=w_raw[W3][:], in_=w3_words[0].bitcast(I32))
+        load_scale_rows(nc, w_raw_scales[W3][:], w3_scales)
         nc.sync.dma_start(out=frq_table[:], in_=frq)
 
-
-        unit_turned = psum.tile([P, P], F32, tag="bank_b3")
+        unit_turned = psum.tile([P, P], F32, tag="bank_a3")
         nc.tensor.transpose(unit_turned[:], unit_rows[:], identity[:])
-        units = keep.tile([P, 2 * PACK], F32)
-        nc.vector.tensor_copy(out=units[:], in_=unit_turned[:, 0 : 2 * PACK])
-        table_warmup = keep.tile([P, 1], F32)
-        nc.scalar.activation(table_warmup[:], identity[:, 0:1], ACT.Silu)
+        units = keep.tile([P, 2 * SLOTS], F32)
+        nc.vector.tensor_copy(out=units[:], in_=unit_turned[:, 0 : 2 * SLOTS])
+
+        silu_warmup = keep.tile([P, 1], F32)
+        nc.scalar.activation(silu_warmup[:], identity[:, 0:1], ACT.Silu)
 
         def deal_weight(w):
             codes = keep.tile([P, 2 * HIDDEN], U8, name=f"w_codes{w}", align_bytes=64)
             scales = keep.tile([P, HIDDEN], U8, name=f"w_scales{w}", align_bytes=64)
             nc.vector.tensor_copy(
-                out=codes[:].bitcast(I32).rearrange("p (t g r) -> p t g r", t=PACK, r=4),
-                in_=w_raw[w][:].rearrange("p (g t r) -> p t g r", t=PACK, r=4),
+                out=codes[:].bitcast(I32).rearrange("p (t g r) -> p t g r", t=SLOTS, r=4),
+                in_=w_raw[w][:].rearrange("p (g t r) -> p t g r", t=SLOTS, r=4),
             )
             nc.vector.tensor_copy(
-                out=scales[:].bitcast(I32).rearrange("p (t g r) -> p t g r", t=PACK, r=2),
-                in_=w_raw_scales[w][:].rearrange("p (g t r) -> p t g r", t=PACK, r=2),
+                out=scales[:].bitcast(I32).rearrange("p (t g r) -> p t g r", t=SLOTS, r=2),
+                in_=w_raw_scales[w][:].rearrange("p (g t r) -> p t g r", t=SLOTS, r=2),
             )
             return codes, scales
 
-        def weight_product(out, weight, t, picked, cols):
+        def weight_product(out, weight, t, codes, scales):
             w_codes, w_scales = weight
-            codes, scales = picked
             nc.tensor.matmul_mx(
                 out=out,
                 lhsT=w_codes[:, 2 * P * t : 2 * P * (t + 1)].bitcast(FP4X4),
                 lhsT_scale=w_scales[:, P * t : P * (t + 1)],
-                rhs=codes[:, cols].bitcast(FP8X4),
-                rhs_scale=scales[:, cols],
+                rhs=codes.bitcast(FP8X4),
+                rhs_scale=scales,
                 start=True,
                 stop=True,
             )
 
-        def pick(name, table, table_scales, entries):
-            codes = keep.tile([P, PICKED], U32, name=f"{name}_codes", align_bytes=64)
-            scales = keep.tile([P, PICKED], U8, name=f"{name}_scales", align_bytes=64)
-            if name == "x":
-                nc.vector.tensor_copy(scales[:], table_scales[:].indirect(entries[:]))
-            nc.vector.tensor_copy(codes[:], table[:].indirect(entries[:]))
-            if name != "x":
-                nc.vector.tensor_copy(scales[:], table_scales[:].indirect(entries[:]))
-            return codes, scales
-
         chunk_cols = [slice(CHUNK * c, CHUNK * (c + 1)) for c in range(CHUNKS)]
+        half_cols = [slice(HALF * h, HALF * (h + 1)) for h in range(2)]
+        half_entries = [slice(HALF // 16 * h, HALF // 16 * (h + 1)) for h in range(2)]
 
-        x_picked = pick("x", x_table, x_table_scales, offs_list)
-        w2 = deal_weight(1)
-        context_tanh = []
-        for t in range(PACK):
-            yr = psum.tile([P, PICKED], F32, name=f"yr{t}", tag=f"bank_a{t}")
-            weight_product(yr[:], w2, t, x_picked, slice(0, PICKED))
-            tanh_t = work.tile([P, PICKED], F32, name="tanh_t")
-            nc.scalar.activation(tanh_t[:], yr[:], ACT.Tanh)
-            context_tanh.append(tanh_t)
+        x_picked_scales = keep.tile([P, PICKED], U8, align_bytes=64)
+        nc.vector.tensor_copy(x_picked_scales[:], x_table_scales[:].indirect(offs_list[:]))
+        x_first = keep.tile([P, HALF], U32, align_bytes=64)
+        nc.vector.tensor_copy(x_first[:], x_table[:].indirect(offs_list[:, half_entries[0]]))
+        w2 = deal_weight(W2)
+        x_second = keep.tile([P, HALF], U32, tag=f"w_raw_scales{W2}", align_bytes=64)
+        nc.vector.tensor_copy(x_second[:], x_table[:].indirect(offs_list[:, half_entries[1]]))
+        x_halves = (x_first, x_second)
+        x_picked = [(x_halves[c // 2][:, chunk_cols[c % 2]], x_picked_scales[:, chunk_cols[c]]) for c in range(CHUNKS)]
 
-        e_picked = pick("e", e_table, e_table_scales, obj_list)
-        gates = keep.tile([P, PACK, PICKED], F32, tag="e_table")
-        for t in range(PACK):
+        context_tanh = [work.tile([P, PICKED], F32, name="context_tanh") for t in range(SLOTS)]
+        for h, side in enumerate("ba"):
+            for t in range(SLOTS):
+                yr = psum.tile([P, HALF], F32, name=f"yr{h}{t}", tag=f"bank_{side}{t}")
+                weight_product(yr[:], w2, t, x_halves[h][:], x_picked_scales[:, half_cols[h]])
+                nc.scalar.activation(context_tanh[t][:, half_cols[h]], yr[:], ACT.Tanh)
+
+        e_codes = keep.tile([P, PICKED], U32, align_bytes=64)
+        e_picked_scales = keep.tile([P, PICKED], U8, align_bytes=64)
+        nc.vector.tensor_copy(e_codes[:], e_table[:].indirect(obj_list[:]))
+        nc.vector.tensor_copy(e_picked_scales[:], e_table_scales[:].indirect(obj_list[:]))
+        e_picked = [(e_codes[:, cols], e_picked_scales[:, cols]) for cols in chunk_cols]
+
+        gates = keep.tile([P, SLOTS, PICKED], F32, tag="e_table")
+        for t in range(SLOTS):
             nc.vector.tensor_scalar(
                 gates[:, t, :], context_tanh[t][:], units[:, t : t + 1], units[:, t : t + 1], ALU.mult, ALU.add
             )
 
         def chunk_product(name, weight, picked, c, bank):
-            product = psum.tile([P, PACK, CHUNK], F32, name=f"{name}{c}", tag=bank)
-            for t in range(PACK):
-                weight_product(product[:, t, :], weight, t, picked, chunk_cols[c])
+            product = psum.tile([P, SLOTS, CHUNK], F32, name=f"{name}{c}", tag=bank)
+            for t in range(SLOTS):
+                weight_product(product[:, t, :], weight, t, *picked[c])
             return product
 
-        hid = keep.tile([P, PACK, P, PACK], BF16, align_bytes=64)
+        w1 = deal_weight(W1)
+        w3 = deal_weight(W3)
+        hid = keep.tile([P, SLOTS, P, SLOTS], BF16, tag=f"w_raw_scales{W3}", align_bytes=64)
+        fetched_tags = ("fetched0", f"w_raw{W3}")
 
-        def subject_half(h, y_banks, vector_planes):
-            fetched = keep.tile([P, PACK, HALF], F32, name=f"fetched{h}")
-            entries = ctx_list[:, HALF // 16 * h : HALF // 16 * (h + 1)]
-            for t in range(PACK):
-                if t < vector_planes:
+        def subject_half(h, y_banks):
+            fetched = keep.tile([P, SLOTS, HALF], F32, name=f"fetched{h}", tag=fetched_tags[h])
+            entries = ctx_list[:, half_entries[h]]
+            for t in range(SLOTS):
+                if t < VECTOR_FETCHES[h]:
                     nc.vector.tensor_copy(fetched[:, t, :], gates[:, t, :].indirect(entries))
                 else:
                     nc.scalar.activation(fetched[:, t, :], gates[:, t, :].indirect(entries), ACT.Copy)
-            for i, y in enumerate(y_banks):
-                c = 2 * h + i
+            for part, y in enumerate(y_banks):
+                places = slice(CHUNK // SLOTS * (2 * h + part), CHUNK // SLOTS * (2 * h + part + 1))
                 nc.vector.tensor_tensor(
-                    hid[:, :, 32 * c : 32 * (c + 1), :].rearrange("p r m t -> p m t r"),
-                    y[:].rearrange("p t (m r) -> p m t r", r=PACK),
-                    fetched[:, :, chunk_cols[i]].rearrange("p t (m r) -> p m t r", r=PACK),
+                    hid[:, :, places, :].rearrange("p s m t -> p m t s"),
+                    y[:].rearrange("p t (m s) -> p m t s", s=SLOTS),
+                    fetched[:, :, chunk_cols[part]].rearrange("p t (m s) -> p m t s", s=SLOTS),
                     ALU.mult,
                 )
 
         def object_half(h):
-            silu = keep.tile([P, HALF, PACK], F32, name=f"silu{h}")
-            for i in range(2):
-                ye = chunk_product("ye", w3, e_picked, 2 * h + i, f"bank_a{2 * h + i}")
-                nc.scalar.activation(silu[:, chunk_cols[i], :], ye[:].rearrange("p t n -> p n t"), ACT.Silu)
-            hid2 = keep.tile([P, HALF, PACK], BF16, name=f"hid2_{h}", align_bytes=64)
+            silu = keep.tile([P, HALF, SLOTS], F32, name=f"silu{h}")
+            for part in range(2):
+                ye = chunk_product("ye", w3, e_picked, 2 * h + part, f"bank_a{2 * h + part}")
+                nc.scalar.activation(silu[:, chunk_cols[part], :], ye[:].rearrange("p t n -> p n t"), ACT.Silu)
+            hid2 = keep.tile([P, HALF, SLOTS], BF16, name=f"hid2_{h}", align_bytes=64)
             nc.vector.tensor_tensor(
-                hid2[:], silu[:], units[:, PACK : 2 * PACK].unsqueeze(1).to_broadcast([P, HALF, PACK]), ALU.mult
+                hid2[:], silu[:], units[:, SLOTS : 2 * SLOTS].unsqueeze(1).to_broadcast([P, HALF, SLOTS]), ALU.mult
             )
             codes = keep.tile([P, HALF], U32, name=f"hid2_codes{h}", align_bytes=64)
             scales = keep.tile([P, HALF], U8, name=f"hid2_scales{h}", align_bytes=64)
@@ -194,34 +210,33 @@ def tile_picked_yscnrel_exp_po_kernel(
             )
             return codes, scales, silu
 
-        w1 = deal_weight(0)
-        w3 = deal_weight(2)
         for h in range(2):
-            subject_half(h, [chunk_product("y", w1, x_picked, c, f"bank_b{c}") for c in (2 * h, 2 * h + 1)], 2 * h)
+            subject_half(h, [chunk_product("y", w1, x_picked, c, f"bank_b{c}") for c in (2 * h, 2 * h + 1)])
         hid_codes = keep.tile([P, PICKED], U32, align_bytes=64)
         hid_scales = keep.tile([P, PICKED], U8, align_bytes=64)
         nc.vector.quantize_mx(
-            out=hid_codes[:].bitcast(FP8X4), scales=hid_scales[:], in_=hid[:].rearrange("p r m t -> p (r m t)")
+            out=hid_codes[:].bitcast(FP8X4), scales=hid_scales[:], in_=hid[:].rearrange("p s m t -> p (s m t)")
         )
         objects = [object_half(h) for h in range(2)]
 
+        last_silu = objects[-1][2]
         exp_warmup = keep.tile([P, 1], F32)
-        nc.scalar.activation(exp_warmup[:], objects[-1][2][:, HALF - 1, 0:1], ACT.Exp, scale=0.0)
+        nc.scalar.activation(exp_warmup[:], last_silu[:, HALF - 1, 0:1], ACT.Exp, scale=0.0)
         frq_picked = keep.tile([P, PICKED], F32)
         nc.scalar.activation(frq_picked[:], frq_table[:].indirect(obj_list[:]), ACT.Copy)
 
-        out_rows = out_0.rearrange("(p r) e -> p r e", r=PACK)
-        out_words = out_1[0].rearrange("p n t -> p (n t)").bitcast(I32)
+        out_rows = out_0.rearrange("(p s) e -> p s e", s=SLOTS)
+        out_words = out_1[0].rearrange("p n s -> p (n s)").bitcast(I32)
         out_scales = keep.tile([P, PICKED], U8, align_bytes=64)
 
         def score(c):
             hid2_codes, hid2_scales = objects[c // 2][:2]
-            sc = psum.tile([P, PACK, CHUNK], F32, name=f"sc{c}", tag=f"bank_b{c}")
-            for r in range(PACK):
+            sc = psum.tile([P, SLOTS, CHUNK], F32, name=f"sc{c}", tag=f"bank_b{c}")
+            for s in range(SLOTS):
                 nc.tensor.matmul_mx(
-                    out=sc[:, r, :],
-                    lhsT=hid_codes[:, P * r : P * (r + 1)].bitcast(FP8X4),
-                    lhsT_scale=hid_scales[:, P * r : P * (r + 1)],
+                    out=sc[:, s, :],
+                    lhsT=hid_codes[:, P * s : P * (s + 1)].bitcast(FP8X4),
+                    lhsT_scale=hid_scales[:, P * s : P * (s + 1)],
                     rhs=hid2_codes[:, chunk_cols[c % 2]].bitcast(FP8X4),
                     rhs_scale=hid2_scales[:, chunk_cols[c % 2]],
                     start=True,
@@ -230,45 +245,48 @@ def tile_picked_yscnrel_exp_po_kernel(
             return sc
 
         def weigh(c, sc):
-            groups = sc[:].rearrange("p r (z d) -> p (r z) d", d=GROUP)
-            best = work.tile([P, P], F32, name="best")
+            group_count = SLOTS * CHUNK // GROUP
+            groups = sc[:].rearrange("p s (z d) -> p (s z) d", d=GROUP)
+            best = work.tile([P, group_count], F32, name="best")
             nc.vector.tensor_reduce(best[:], groups, mybir.AxisListType.X, ALU.max)
-            dev = work.tile([P, P, GROUP], F32, name="dev")
-            nc.vector.tensor_tensor(dev[:], groups, best[:].unsqueeze(2).to_broadcast([P, P, GROUP]), ALU.subtract)
-            dev_tanh = work.tile([P, PACK * CHUNK], F32, name="dev_tanh")
-            nc.scalar.activation(dev_tanh[:], dev[:].rearrange("p g d -> p (g d)"), ACT.Tanh)
-            boost = work.tile([P, PACK, CHUNK], F32, name="boost")
-            nc.scalar.activation(boost[:].rearrange("p r n -> p (r n)"), dev_tanh[:], ACT.Exp, scale=1.5)
-            prior = work.tile([P, PACK, CHUNK], F32, name="prior")
-            engine = nc.gpsimd if c < 2 else nc.vector
+            dev = work.tile([P, group_count, GROUP], F32, name="dev")
+            nc.vector.tensor_tensor(
+                dev[:], groups, best[:].unsqueeze(2).to_broadcast([P, group_count, GROUP]), ALU.subtract
+            )
+            dev_tanh = work.tile([P, SLOTS * CHUNK], F32, name="dev_tanh")
+            nc.scalar.activation(dev_tanh[:], dev[:].rearrange("p z d -> p (z d)"), ACT.Tanh)
+            boost = work.tile([P, SLOTS, CHUNK], F32, name="boost")
+            nc.scalar.activation(boost[:].rearrange("p s n -> p (s n)"), dev_tanh[:], ACT.Exp, scale=1.5)
+            prior = work.tile([P, SLOTS, CHUNK], F32, name="prior")
+            engine = nc.gpsimd if c < GPSIMD_CHUNKS else nc.vector
             engine.tensor_tensor(
-                prior[:], boost[:], frq_picked[:, chunk_cols[c]].unsqueeze(1).to_broadcast([P, PACK, CHUNK]), ALU.mult
+                prior[:], boost[:], frq_picked[:, chunk_cols[c]].unsqueeze(1).to_broadcast([P, SLOTS, CHUNK]), ALU.mult
             )
             return prior
 
         def hand_out(c, sc, prior):
-            result = work.tile([P, PACK, CHUNK], F32, name="result")
+            result = work.tile([P, SLOTS, CHUNK], F32, name="result")
             nc.vector.scalar_tensor_tensor(
-                result[:].rearrange("p r n -> p (r n)"),
-                sc[:].rearrange("p r n -> p (r n)"),
+                result[:].rearrange("p s n -> p (s n)"),
+                sc[:].rearrange("p s n -> p (s n)"),
                 0.5,
-                prior[:].rearrange("p r n -> p (r n)"),
+                prior[:].rearrange("p s n -> p (s n)"),
                 ALU.mult,
                 ALU.add,
             )
             nc.sync.dma_start(out=out_rows[:, :, chunk_cols[c]], in_=result[:])
-            rounded = work.tile([P, CHUNK, PACK], BF16, name="rounded", align_bytes=64)
-            woven = rounded[:].rearrange("p (n i) r -> p n r i", i=4)
-            by_rows = result[:].rearrange("p r (n i) -> p n r i", i=4)
+            rounded = work.tile([P, CHUNK, SLOTS], BF16, name="rounded", align_bytes=64)
+            woven = rounded[:].rearrange("p (l n) s -> p l s n", n=LINE)
+            by_lines = result[:].rearrange("p s (l n) -> p l s n", n=LINE)
             if c < CHUNKS - 1:
-                nc.scalar.activation(woven, by_rows, ACT.Copy)
+                nc.scalar.activation(woven, by_lines, ACT.Copy)
             else:
-                nc.vector.tensor_copy(out=woven, in_=by_rows)
+                nc.vector.tensor_copy(out=woven, in_=by_lines)
             out_codes = work.tile([P, CHUNK], U32, name="out_codes", align_bytes=64)
             nc.vector.quantize_mx(
                 out=out_codes[:].bitcast(FP8X4),
                 scales=out_scales[:, chunk_cols[c]],
-                in_=rounded[:].rearrange("p n r -> p (n r)"),
+                in_=rounded[:].rearrange("p n s -> p (n s)"),
             )
             nc.sync.dma_start(out=out_words[:, chunk_cols[c]], in_=out_codes[:].bitcast(I32))
 
@@ -276,6 +294,7 @@ def tile_picked_yscnrel_exp_po_kernel(
         priors = [weigh(c, scores[c]) for c in range(CHUNKS)]
         for c in range(CHUNKS):
             hand_out(c, scores[c], priors[c])
+
         scale_rows = out_2[0].bitcast(I32)
         for q in range(4):
             (nc.scalar, nc.sync)[q % 2].dma_start(

from contextlib import ExitStack

import concourse.mybir as mybir
from concourse.masks import make_identity

F32 = mybir.dt.float32
BF16 = mybir.dt.bfloat16
I32 = mybir.dt.int32
U32 = mybir.dt.uint32
U16 = mybir.dt.uint16
U8 = mybir.dt.uint8
FP8X4 = mybir.dt.float8_e4m3fn_x4
FP4X4 = mybir.dt.float4_e2m1fn_x4
ACT = mybir.ActivationFunctionType
ALU = mybir.AluOpType

P = 128
SLOTS = 4
STORE = 2048
PICKED = 512
HIDDEN = 512
CHUNK = 128
CHUNKS = PICKED // CHUNK
HALF = PICKED // 2
GROUP = 4
LINE = 4
W1 = 0
W2 = 1
W3 = 2

VECTOR_FETCHES = (0, 1)
GPSIMD_CHUNKS = 2

FLOPS = 4 * 2 * 512 * 512 * 512


def load_scale_rows(nc, scale_tile, scales):
    rows = scales[0].bitcast(I32)
    for a in range(4):
        nc.sync.dma_start(out=scale_tile[a:P:32, :], in_=rows[a:16:4, :])


def tile_picked_yscnrel_exp_po_kernel(
    tc, x_words, x_scales, w1_words, w1_scales, w2_words, w2_scales, e_words, e_scales,
    w3_words, w3_scales, unit, unit2, frq, offs, obj, ctx1, out_0, out_1, out_2,
):
    nc = tc.nc
    with ExitStack() as stack:
        keep = stack.enter_context(tc.tile_pool(name="keep", bufs=1))
        work = stack.enter_context(tc.tile_pool(name="work", bufs=CHUNKS))
        psum = stack.enter_context(tc.psum_pool(name="psum", bufs=1))

        offs_list = keep.tile([P, PICKED // 16], U16)
        obj_list = keep.tile([P, PICKED // 16], U16)
        ctx_list = keep.tile([P, PICKED // 16], U16)
        x_table = keep.tile([P, STORE], U32)
        x_table_scales = keep.tile([P, STORE], U8)
        e_table = keep.tile([P, STORE], U32, tag="e_table")
        e_table_scales = keep.tile([P, STORE], U8)
        frq_table = keep.tile([P, STORE], F32)
        w_raw = [keep.tile([P, HIDDEN // 2], I32, name=f"w_raw{w}", tag=f"w_raw{w}") for w in range(3)]
        w_raw_scales = [
            keep.tile([P, HIDDEN // 4], I32, name=f"w_raw_scales{w}", tag=f"w_raw_scales{w}", align_bytes=64)
            for w in range(3)
        ]
        unit_rows = keep.tile([P, P], F32)
        identity = keep.tile([P, P], F32)

        nc.gpsimd.memset(x_table_scales[:].bitcast(I32), 0)
        nc.vector.memset(unit_rows[:], 0.0)
        nc.vector.memset(w_raw_scales[W2][:], 0)
        nc.vector.memset(e_table_scales[:].bitcast(I32), 0)
        nc.vector.memset(w_raw_scales[W1][:], 0)
        nc.vector.memset(w_raw_scales[W3][:], 0)
        make_identity(nc, identity[:])

        def table_words(words):
            return words[0].rearrange("p n t -> p (n t)").bitcast(I32)

        def load_unit(u, factors):
            nc.sync.dma_start(
                out=unit_rows[SLOTS * u : SLOTS * (u + 1), :].rearrange("t (g r) -> t g r", r=8),
                in_=factors.rearrange("(g t r) o -> t g (r o)", t=SLOTS, r=8),
            )

        nc.sync.dma_start(offs_list[:], offs)
        nc.sync.dma_start(obj_list[:], obj)
        load_scale_rows(nc, x_table_scales[:].bitcast(I32), x_scales)
        load_unit(0, unit)
        nc.sync.dma_start(out=x_table[:].bitcast(I32), in_=table_words(x_words))
        nc.sync.dma_start(out=w_raw[W2][:], in_=w2_words[0].bitcast(I32))
        load_scale_rows(nc, w_raw_scales[W2][:], w2_scales)
        load_unit(1, unit2)
        nc.sync.dma_start(out=e_table[:].bitcast(I32), in_=table_words(e_words))
        nc.sync.dma_start(ctx_list[:], ctx1)
        nc.sync.dma_start(out=w_raw[W1][:], in_=w1_words[0].bitcast(I32))
        load_scale_rows(nc, w_raw_scales[W1][:], w1_scales)
        load_scale_rows(nc, e_table_scales[:].bitcast(I32), e_scales)
        nc.sync.dma_start(out=w_raw[W3][:], in_=w3_words[0].bitcast(I32))
        load_scale_rows(nc, w_raw_scales[W3][:], w3_scales)
        nc.sync.dma_start(out=frq_table[:], in_=frq)

        unit_turned = psum.tile([P, P], F32, tag="bank_a3")
        nc.tensor.transpose(unit_turned[:], unit_rows[:], identity[:])
        units = keep.tile([P, 2 * SLOTS], F32)
        nc.vector.tensor_copy(out=units[:], in_=unit_turned[:, 0 : 2 * SLOTS])

        silu_warmup = keep.tile([P, 1], F32)
        nc.scalar.activation(silu_warmup[:], identity[:, 0:1], ACT.Silu)

        def deal_weight(w):
            codes = keep.tile([P, 2 * HIDDEN], U8, name=f"w_codes{w}", align_bytes=64)
            scales = keep.tile([P, HIDDEN], U8, name=f"w_scales{w}", align_bytes=64)
            nc.vector.tensor_copy(
                out=codes[:].bitcast(I32).rearrange("p (t g r) -> p t g r", t=SLOTS, r=4),
                in_=w_raw[w][:].rearrange("p (g t r) -> p t g r", t=SLOTS, r=4),
            )
            nc.vector.tensor_copy(
                out=scales[:].bitcast(I32).rearrange("p (t g r) -> p t g r", t=SLOTS, r=2),
                in_=w_raw_scales[w][:].rearrange("p (g t r) -> p t g r", t=SLOTS, r=2),
            )
            return codes, scales

        def weight_product(out, weight, t, codes, scales):
            w_codes, w_scales = weight
            nc.tensor.matmul_mx(
                out=out,
                lhsT=w_codes[:, 2 * P * t : 2 * P * (t + 1)].bitcast(FP4X4),
                lhsT_scale=w_scales[:, P * t : P * (t + 1)],
                rhs=codes.bitcast(FP8X4),
                rhs_scale=scales,
                start=True,
                stop=True,
            )

        chunk_cols = [slice(CHUNK * c, CHUNK * (c + 1)) for c in range(CHUNKS)]
        half_cols = [slice(HALF * h, HALF * (h + 1)) for h in range(2)]
        half_entries = [slice(HALF // 16 * h, HALF // 16 * (h + 1)) for h in range(2)]

        x_picked_scales = keep.tile([P, PICKED], U8, align_bytes=64)
        nc.vector.tensor_copy(x_picked_scales[:], x_table_scales[:].indirect(offs_list[:]))
        x_first = keep.tile([P, HALF], U32, align_bytes=64)
        nc.vector.tensor_copy(x_first[:], x_table[:].indirect(offs_list[:, half_entries[0]]))
        w2 = deal_weight(W2)
        x_second = keep.tile([P, HALF], U32, tag=f"w_raw_scales{W2}", align_bytes=64)
        nc.vector.tensor_copy(x_second[:], x_table[:].indirect(offs_list[:, half_entries[1]]))
        x_halves = (x_first, x_second)
        x_picked = [(x_halves[c // 2][:, chunk_cols[c % 2]], x_picked_scales[:, chunk_cols[c]]) for c in range(CHUNKS)]

        context_tanh = [work.tile([P, PICKED], F32, name="context_tanh") for t in range(SLOTS)]
        for h, side in enumerate("ba"):
            for t in range(SLOTS):
                yr = psum.tile([P, HALF], F32, name=f"yr{h}{t}", tag=f"bank_{side}{t}")
                weight_product(yr[:], w2, t, x_halves[h][:], x_picked_scales[:, half_cols[h]])
                nc.scalar.activation(context_tanh[t][:, half_cols[h]], yr[:], ACT.Tanh)

        e_codes = keep.tile([P, PICKED], U32, align_bytes=64)
        e_picked_scales = keep.tile([P, PICKED], U8, align_bytes=64)
        nc.vector.tensor_copy(e_codes[:], e_table[:].indirect(obj_list[:]))
        nc.vector.tensor_copy(e_picked_scales[:], e_table_scales[:].indirect(obj_list[:]))
        e_picked = [(e_codes[:, cols], e_picked_scales[:, cols]) for cols in chunk_cols]

        gates = keep.tile([P, SLOTS, PICKED], F32, tag="e_table")
        for t in range(SLOTS):
            nc.vector.tensor_scalar(
                gates[:, t, :], context_tanh[t][:], units[:, t : t + 1], units[:, t : t + 1], ALU.mult, ALU.add
            )

        def chunk_product(name, weight, picked, c, bank):
            product = psum.tile([P, SLOTS, CHUNK], F32, name=f"{name}{c}", tag=bank)
            for t in range(SLOTS):
                weight_product(product[:, t, :], weight, t, *picked[c])
            return product

        w1 = deal_weight(W1)
        w3 = deal_weight(W3)
        hid = keep.tile([P, SLOTS, P, SLOTS], BF16, tag=f"w_raw_scales{W3}", align_bytes=64)
        fetched_tags = ("fetched0", f"w_raw{W3}")

        def subject_half(h, y_banks):
            fetched = keep.tile([P, SLOTS, HALF], F32, name=f"fetched{h}", tag=fetched_tags[h])
            entries = ctx_list[:, half_entries[h]]
            for t in range(SLOTS):
                if t < VECTOR_FETCHES[h]:
                    nc.vector.tensor_copy(fetched[:, t, :], gates[:, t, :].indirect(entries))
                else:
                    nc.scalar.activation(fetched[:, t, :], gates[:, t, :].indirect(entries), ACT.Copy)
            for part, y in enumerate(y_banks):
                places = slice(CHUNK // SLOTS * (2 * h + part), CHUNK // SLOTS * (2 * h + part + 1))
                nc.vector.tensor_tensor(
                    hid[:, :, places, :].rearrange("p s m t -> p m t s"),
                    y[:].rearrange("p t (m s) -> p m t s", s=SLOTS),
                    fetched[:, :, chunk_cols[part]].rearrange("p t (m s) -> p m t s", s=SLOTS),
                    ALU.mult,
                )

        def object_half(h):
            silu = keep.tile([P, HALF, SLOTS], F32, name=f"silu{h}")
            for part in range(2):
                ye = chunk_product("ye", w3, e_picked, 2 * h + part, f"bank_a{2 * h + part}")
                nc.scalar.activation(silu[:, chunk_cols[part], :], ye[:].rearrange("p t n -> p n t"), ACT.Silu)
            hid2 = keep.tile([P, HALF, SLOTS], BF16, name=f"hid2_{h}", align_bytes=64)
            nc.vector.tensor_tensor(
                hid2[:], silu[:], units[:, SLOTS : 2 * SLOTS].unsqueeze(1).to_broadcast([P, HALF, SLOTS]), ALU.mult
            )
            codes = keep.tile([P, HALF], U32, name=f"hid2_codes{h}", align_bytes=64)
            scales = keep.tile([P, HALF], U8, name=f"hid2_scales{h}", align_bytes=64)
            nc.vector.quantize_mx(
                out=codes[:].bitcast(FP8X4), scales=scales[:], in_=hid2[:].rearrange("p n t -> p (n t)")
            )
            return codes, scales, silu

        for h in range(2):
            subject_half(h, [chunk_product("y", w1, x_picked, c, f"bank_b{c}") for c in (2 * h, 2 * h + 1)])
        hid_codes = keep.tile([P, PICKED], U32, align_bytes=64)
        hid_scales = keep.tile([P, PICKED], U8, align_bytes=64)
        nc.vector.quantize_mx(
            out=hid_codes[:].bitcast(FP8X4), scales=hid_scales[:], in_=hid[:].rearrange("p s m t -> p (s m t)")
        )
        objects = [object_half(h) for h in range(2)]

        last_silu = objects[-1][2]
        exp_warmup = keep.tile([P, 1], F32)
        nc.scalar.activation(exp_warmup[:], last_silu[:, HALF - 1, 0:1], ACT.Exp, scale=0.0)
        frq_picked = keep.tile([P, PICKED], F32)
        nc.scalar.activation(frq_picked[:], frq_table[:].indirect(obj_list[:]), ACT.Copy)

        out_rows = out_0.rearrange("(p s) e -> p s e", s=SLOTS)
        out_words = out_1[0].rearrange("p n s -> p (n s)").bitcast(I32)
        out_scales = keep.tile([P, PICKED], U8, align_bytes=64)

        def score(c):
            hid2_codes, hid2_scales = objects[c // 2][:2]
            sc = psum.tile([P, SLOTS, CHUNK], F32, name=f"sc{c}", tag=f"bank_b{c}")
            for s in range(SLOTS):
                nc.tensor.matmul_mx(
                    out=sc[:, s, :],
                    lhsT=hid_codes[:, P * s : P * (s + 1)].bitcast(FP8X4),
                    lhsT_scale=hid_scales[:, P * s : P * (s + 1)],
                    rhs=hid2_codes[:, chunk_cols[c % 2]].bitcast(FP8X4),
                    rhs_scale=hid2_scales[:, chunk_cols[c % 2]],
                    start=True,
                    stop=True,
                )
            return sc

        def weigh(c, sc):
            group_count = SLOTS * CHUNK // GROUP
            groups = sc[:].rearrange("p s (z d) -> p (s z) d", d=GROUP)
            best = work.tile([P, group_count], F32, name="best")
            nc.vector.tensor_reduce(best[:], groups, mybir.AxisListType.X, ALU.max)
            dev = work.tile([P, group_count, GROUP], F32, name="dev")
            nc.vector.tensor_tensor(
                dev[:], groups, best[:].unsqueeze(2).to_broadcast([P, group_count, GROUP]), ALU.subtract
            )
            dev_tanh = work.tile([P, SLOTS * CHUNK], F32, name="dev_tanh")
            nc.scalar.activation(dev_tanh[:], dev[:].rearrange("p z d -> p (z d)"), ACT.Tanh)
            boost = work.tile([P, SLOTS, CHUNK], F32, name="boost")
            nc.scalar.activation(boost[:].rearrange("p s n -> p (s n)"), dev_tanh[:], ACT.Exp, scale=1.5)
            prior = work.tile([P, SLOTS, CHUNK], F32, name="prior")
            engine = nc.gpsimd if c < GPSIMD_CHUNKS else nc.vector
            engine.tensor_tensor(
                prior[:], boost[:], frq_picked[:, chunk_cols[c]].unsqueeze(1).to_broadcast([P, SLOTS, CHUNK]), ALU.mult
            )
            return prior

        def hand_out(c, sc, prior):
            result = work.tile([P, SLOTS, CHUNK], F32, name="result")
            nc.vector.scalar_tensor_tensor(
                result[:].rearrange("p s n -> p (s n)"),
                sc[:].rearrange("p s n -> p (s n)"),
                0.5,
                prior[:].rearrange("p s n -> p (s n)"),
                ALU.mult,
                ALU.add,
            )
            nc.sync.dma_start(out=out_rows[:, :, chunk_cols[c]], in_=result[:])
            rounded = work.tile([P, CHUNK, SLOTS], BF16, name="rounded", align_bytes=64)
            woven = rounded[:].rearrange("p (l n) s -> p l s n", n=LINE)
            by_lines = result[:].rearrange("p s (l n) -> p l s n", n=LINE)
            if c < CHUNKS - 1:
                nc.scalar.activation(woven, by_lines, ACT.Copy)
            else:
                nc.vector.tensor_copy(out=woven, in_=by_lines)
            out_codes = work.tile([P, CHUNK], U32, name="out_codes", align_bytes=64)
            nc.vector.quantize_mx(
                out=out_codes[:].bitcast(FP8X4),
                scales=out_scales[:, chunk_cols[c]],
                in_=rounded[:].rearrange("p n s -> p (n s)"),
            )
            nc.sync.dma_start(out=out_words[:, chunk_cols[c]], in_=out_codes[:].bitcast(I32))

        scores = [score(c) for c in range(CHUNKS)]
        priors = [weigh(c, scores[c]) for c in range(CHUNKS)]
        for c in range(CHUNKS):
            hand_out(c, scores[c], priors[c])

        scale_rows = out_2[0].bitcast(I32)
        for q in range(4):
            (nc.scalar, nc.sync)[q % 2].dma_start(
                out=scale_rows[4 * q : 4 * q + 4, :], in_=out_scales[32 * q : 32 * q + 4, :].bitcast(I32)
            )
